import numpy as np
import ml_dtypes


def mxq(x, axis, fmt="e4m3"):
    dtype, down = {"e4m3": (ml_dtypes.float8_e4m3fn, 7), "e5m2": (ml_dtypes.float8_e5m2, 14)}[fmt]
    v = np.moveaxis(np.asarray(x, np.float32).astype(ml_dtypes.bfloat16).astype(np.float64), axis, -1)
    blocks = v.reshape(v.shape[:-1] + (-1, 32))
    amax = np.abs(blocks).max(-1, keepdims=True)
    byte = np.maximum(np.where(amax > 0, np.frexp(amax)[1] - 1 + 127, 0) - down, 1)
    scale = np.exp2(byte - 127.0)
    codes = (blocks / scale).astype(np.float32).astype(dtype).astype(np.float64)
    return np.moveaxis((codes * scale).reshape(v.shape), -1, axis)


WIDE = False


def mx_kscale(k):
    if not WIDE:
        return np.ones(k)
    levels = np.array([30, -30])
    if k % 512:
        return np.exp2(np.random.permutation(np.resize(levels, k // 32))).repeat(32)
    a = np.empty((k // 512, 16))
    for p in range(k // 512):
        a[p, :8] = np.random.permutation(np.resize(levels, 8))
        for g in range(8):
            far = levels[np.abs(levels - a[p, g]) >= 10]
            a[p, g + 8] = far[np.random.randint(len(far))]
    return np.exp2(a.ravel()).repeat(32)


def f64(x):
    return np.asarray(x).astype(np.float64)


def striped(idx):
    return np.tile(np.asarray(idx).reshape(-1, 16).T, (8, 1)).astype(np.uint16)


def unstriped(offs):
    return offs[:16].T.reshape(-1).astype(np.int64)


E2M1 = np.array([0.0, 0.5, 1.0, 1.5, 2.0, 3.0, 4.0, 6.0, -0.0, -0.5, -1.0, -1.5, -2.0, -3.0, -4.0, -6.0])


def pack_weight(w, fmt):
    k, n = w.shape
    w = f64(np.asarray(w, np.float32).astype(ml_dtypes.bfloat16)).reshape(k // 32, 32, n)
    amax = np.abs(w).max(1)
    if fmt == "e4m3":
        byte = np.frexp(amax)[1] - 1 + 127 - 7
    else:
        mant, ex = np.frexp(amax / 6.0)
        byte = np.where(mant > 0.5, ex, ex - 1) + 127
    byte = np.clip(np.where(amax > 0, byte, 1), 1, 254)
    scaled = (w * np.exp2(127.0 - byte)[:, None, :]).reshape(k, n).astype(np.float32)
    by_word = np.ascontiguousarray(scaled.reshape(k // 512, 128, 4, n).transpose(0, 1, 3, 2))
    if fmt == "e4m3":
        words = by_word.astype(ml_dtypes.float8_e4m3fn).view(np.uint8)
    else:
        c = by_word.astype(ml_dtypes.float4_e2m1fn).view(np.uint8) & 0xF
        words = (c[..., 0::2] | (c[..., 1::2] << 4)).reshape(k // 512, 128, 2 * n)
    return np.ascontiguousarray(words), np.ascontiguousarray(byte.astype(np.uint8).reshape(k // 512, 16, n))


def unpack_weight(words, scales, fmt):
    g, _, n = scales.shape
    words = np.ascontiguousarray(words).reshape(g, 128, n, -1)
    if fmt == "e4m3":
        vals = words.view(ml_dtypes.float8_e4m3fn).astype(np.float64)
    else:
        nib = np.empty((g, 128, n, 4), np.uint8)
        nib[..., 0::2] = words & 0xF
        nib[..., 1::2] = words >> 4
        vals = E2M1[nib]
    vals = vals * np.repeat(np.exp2(scales.astype(np.float64) - 127.0), 8, axis=1)[..., None]
    return vals.transpose(0, 1, 3, 2).reshape(g * 512, n)


def bf(x):
    return np.asarray(x, np.float32).astype(ml_dtypes.bfloat16)


def planes(Y):
    r, m = Y.shape
    b = f64(bf(Y)).reshape(r // 32, 32, m)
    amax = np.abs(b).max(1)
    byte = np.clip(np.where(amax > 0, np.frexp(amax)[1] - 1 + 127 - 7, 1), 1, 254)
    codes = (b * np.exp2(127.0 - byte)[:, None, :]).reshape(r, m).astype(np.float32).astype(ml_dtypes.float8_e4m3fn).view(np.uint8)
    words = codes.reshape(r // 512, 128, 4, m).transpose(0, 1, 3, 2)
    return np.ascontiguousarray(words), np.ascontiguousarray(byte.astype(np.uint8).reshape(r // 512, 16, m))


K, T, J, R, C, O, N = 1024, 1024, 256, 512, 1024, 256, 512


def setup_inputs():
    n = np.random.standard_normal
    idx = np.random.permutation(T)[:J]
    idx2 = np.random.permutation(T)[:J]
    idx3 = np.random.permutation(C)[:J]
    idx4 = np.random.permutation(C)[:O]
    fk = mx_kscale(K)
    fr = mx_kscale(R)
    wp = pack_weight(n((K, R)) * 1 / np.sqrt(K) * fk[:, None] * fr, "e4m3")
    wbp = pack_weight(n((R, N)) * 1 / np.sqrt(R) / fr[:, None], "e2m1")
    return {
        "xf": (n((K, T))).astype(np.float32),
        "fk": (np.random.uniform(0.5, 2.0, (K, 1)) / fk[:, None]).astype(np.float32),
        "w_words": wp[0],
        "w_scales": wp[1],
        "oldh": (n((R, C)) * 0.7 * fr[:, None]).astype(np.float32),
        "wb_words": wbp[0],
        "wb_scales": wbp[1],
        "rs": (n((N, O))).astype(np.float32),
        "gm": (np.random.uniform(0.5, 2.0, (N, 1))).astype(np.float32),
        "offs": striped(idx),
        "offs2": striped(idx2),
        "offs3": striped(idx3),
        "offs4": striped(idx4),
    }


def reference(xf, fk, w_words, w_scales, oldh, wb_words, wb_scales, rs, gm, offs, offs2, offs3, offs4):
    idx = unstriped(offs)
    idx2 = unstriped(offs2)
    idx3 = unstriped(offs3)
    idx4 = unstriped(offs4)
    wu = unpack_weight(w_words, w_scales, "e4m3")
    wbu = unpack_weight(wb_words, wb_scales, "e2m1")
    u = np.maximum(f64(xf)[:, idx], f64(xf)[:, idx2]) * f64(fk)
    uq = mxq(u, 0, "e4m3")
    a = wu.T @ uq
    ha = np.maximum(a, 0.0)
    pw0 = np.zeros((R, C))
    pw0[:, idx3] = ha
    pg = pw0 + f64(oldh)
    hid = pg[:, idx4]
    hidq = mxq(hid, 0, "e5m2")
    p = wbu.T @ hidq
    y = f64(gm) * p + f64(rs)
    words, scales = planes(y)
    return y, words, scales

@@ -1,0 +1,240 @@
+from contextlib import ExitStack
+
+import concourse.mybir as mybir
+
+K, T, J, R, C, O, N = 1024, 1024, 256, 512, 1024, 256, 512
+FLOPS = 2 * K * R * J + 2 * R * N * O
+
+F32 = mybir.dt.float32
+BF16 = mybir.dt.bfloat16
+I32 = mybir.dt.int32
+U32 = mybir.dt.uint32
+U16 = mybir.dt.uint16
+U8 = mybir.dt.uint8
+E4M3 = mybir.dt.float8_e4m3fn_x4
+E5M2 = mybir.dt.float8_e5m2_x4
+E2M1 = mybir.dt.float4_e2m1fn_x4
+ALU = mybir.AluOpType
+ACT = mybir.ActivationFunctionType
+
+P = 128
+PACK = 4
+PASSES = K // (P * PACK)
+QUADS = 4
+WB_ROW, W_ROW = 96, 112
+VECTOR_PICKS = (0, 1, 2, 3, 5, 6)
+
+
+def interleave(nc, dst, src):
+    nc.vector.tensor_copy(
+        out=dst[:].rearrange("p (c i) t -> p c t i", i=4),
+        in_=src[:].rearrange("p t (c i) -> p c t i", i=4),
+    )
+
+
+def tile_list_page_largerpicks_residual_pl_kernel(
+    tc, xf, fk, w_words, w_scales, oldh, wb_words, wb_scales, rs, gm, offs, offs2, offs3, offs4, out_0, out_1, out_2
+):
+    nc = tc.nc
+    with ExitStack() as ctx:
+        lists = ctx.enter_context(tc.tile_pool(name="lists", bufs=1))
+        keep = ctx.enter_context(tc.tile_pool(name="keep", bufs=1))
+        psum = ctx.enter_context(tc.psum_pool(name="psum", bufs=1))
+
+        def held(shape, dtype, name):
+            return keep.tile(shape, dtype, name=name, align_bytes=64)
+
+        first = lists.tile([P, J // 16], U16, name="first")
+        second = lists.tile([P, J // 16], U16, name="second")
+        put = lists.tile([P, J // 16], U16, name="put")
+        read = lists.tile([P, O // 16], U16, name="read")
+
+        rows_raw = held([P, PASSES * R], U8, "rows_raw")
+        nc.vector.memset(rows_raw[0:WB_ROW, :].bitcast(U32), 0)
+        nc.vector.memset(rows_raw[WB_ROW:W_ROW, N:].bitcast(U32), 0)
+        nc.sync.dma_start(first[:], offs)
+        nc.sync.dma_start(second[:], offs2)
+        wb_raw = held([P, N], U16, "wb_raw")
+        nc.scalar.dma_start(wb_raw[:].bitcast(I32), wb_words[0].bitcast(I32))
+        nc.scalar.dma_start(
+            rows_raw[W_ROW:P, :].bitcast(I32).rearrange("q (a c) -> q a c", a=PASSES),
+            w_scales.bitcast(I32).rearrange("a q c -> q a c"),
+        )
+        nc.scalar.dma_start(rows_raw[WB_ROW:W_ROW, 0:N].bitcast(I32), wb_scales[0].bitcast(I32))
+        fk_sb = held([P, PASSES, PACK], F32, "fk_sb")
+        nc.scalar.dma_start(fk_sb[:], fk.rearrange("(a p t) o -> p a (t o)", p=P, t=PACK))
+        ws = held([P, PASSES * R], U8, "ws")
+        wbs = held([P, N], U8, "wbs")
+        nc.gpsimd.memset(ws[:].bitcast(U32), 0)
+        nc.gpsimd.memset(wbs[:].bitcast(U32), 0)
+        x_rows = xf.rearrange("(a p t) c -> a t p c", p=P, t=PACK)
+        x_tiles = []
+        for i in range(PASSES * PACK):
+            x_tile = held([P, T], F32, "x%d" % i)
+            nc.sync.dma_start(x_tile[:], x_rows[i // PACK, i % PACK])
+            x_tiles.append(x_tile)
+
+        placed = []
+        for t in range(PACK):
+            placed_tile = held([P, C], F32, "placed%d" % t)
+            (nc.vector if t < 2 else nc.gpsimd).memset(placed_tile[:], 0.0)
+            placed.append(placed_tile)
+
+        wb_dealt = held([P, N], U16, "wb_dealt")
+        nc.scalar.copy(
+            out=wb_dealt[:].rearrange("p (t m) -> p m t", t=PACK),
+            in_=wb_raw[:].rearrange("p (m t) -> p m t", t=PACK),
+        )
+        rows_dealt = held([P, PASSES * R], U8, "rows_dealt")
+        nc.vector.tensor_copy(
+            out=rows_dealt[:].rearrange("p (a t m) -> p a m t", a=PASSES, t=PACK),
+            in_=rows_raw[:].rearrange("p (a m t) -> p a m t", a=PASSES, t=PACK),
+        )
+        for q in range(QUADS):
+            nc.sync.dma_start(
+                ws[32 * q : 32 * q + 4, :].bitcast(I32), rows_dealt[W_ROW + 4 * q : W_ROW + 4 * q + 4, :].bitcast(I32)
+            )
+        w_raw = []
+        for a in range(PASSES):
+            w_tile = held([P, R], U32, "w_raw%d" % a)
+            nc.sync.dma_start(w_tile[:].bitcast(I32), w_words[a].rearrange("p c r -> p (c r)").bitcast(I32))
+            w_raw.append(w_tile)
+        nc.sync.dma_start(put[:], offs3)
+        old_rows = oldh.rearrange("(p t) c -> t p c", t=PACK)
+        old = []
+        for t in range(PACK):
+            old_tile = held([P, C], F32, "old%d" % t)
+            nc.sync.dma_start(old_tile[:], old_rows[t])
+            old.append(old_tile)
+        nc.sync.dma_start(read[:], offs4)
+        for q in range(QUADS):
+            nc.sync.dma_start(
+                wbs[32 * q : 32 * q + 4, :].bitcast(I32), rows_dealt[WB_ROW + 4 * q : WB_ROW + 4 * q + 4, 0:N].bitcast(I32)
+            )
+
+        gm_sb = held([P, PACK], F32, "gm_sb")
+        nc.sync.dma_start(gm_sb[:], gm.rearrange("(p t) o -> p (t o)", t=PACK))
+        rs_sb = held([P, PACK, O], F32, "rs_sb")
+        nc.sync.dma_start(rs_sb[:], rs.rearrange("(p t) o -> p t o", t=PACK))
+
+        u_codes, u_scales = [], []
+        for a in range(PASSES):
+            u_bf = held([P, J, PACK], BF16, "u_bf%d" % a)
+            pick1 = held([P, PACK, J], F32, "pick1_%d" % a)
+            pick2 = held([P, PACK, J], F32, "pick2_%d" % a)
+            larger = held([P, PACK, J], F32, "larger%d" % a)
+            last = a == PASSES - 1
+            max_groups = ((0, 2), (2, 3), (3, 4)) if last else ((0, 2), (2, 4))
+            joint = PACK - 1 if last else PACK
+            for lo, hi in max_groups:
+                for t in range(lo, hi):
+                    i = a * PACK + t
+                    nc.scalar.activation(pick1[:, t, :], x_tiles[i][:].indirect(first[:]), ACT.Copy)
+                    if i in VECTOR_PICKS:
+                        nc.vector.tensor_copy(pick2[:, t, :], x_tiles[i][:].indirect(second[:]))
+                    else:
+                        nc.scalar.activation(pick2[:, t, :], x_tiles[i][:].indirect(second[:]), ACT.Copy)
+                nc.vector.tensor_tensor(larger[:, lo:hi, :], pick1[:, lo:hi, :], pick2[:, lo:hi, :], ALU.max)
+                if hi == joint:
+                    nc.vector.tensor_tensor(
+                        u_bf[:, :, 0:joint].rearrange("p (c i) t -> p c t i", i=4),
+                        larger[:, 0:joint, :].rearrange("p t (c i) -> p c t i", i=4),
+                        fk_sb[:, a, 0:joint].unsqueeze(1).unsqueeze(3).to_broadcast([P, J // 4, joint, 4]),
+                        ALU.mult,
+                    )
+                elif hi > joint:
+                    nc.vector.tensor_scalar(u_bf[:, :, lo], larger[:, lo, :], fk_sb[:, a, lo:hi], None, ALU.mult)
+            codes = held([P, J], U32, "u_codes%d" % a)
+            scales = held([P, J], U8, "u_scales%d" % a)
+            nc.vector.quantize_mx(
+                out=codes[:].bitcast(E4M3), scales=scales[:], in_=u_bf[:].rearrange("p j t -> p (j t)")
+            )
+            u_codes.append(codes)
+            u_scales.append(scales)
+
+        w_dealt = []
+        for a in range(PASSES):
+            dealt = held([P, R], U32, "w_dealt%d" % a)
+            nc.scalar.copy(
+                out=dealt[:].rearrange("p (t m) -> p m t", t=PACK),
+                in_=w_raw[a][:].rearrange("p (m t) -> p m t", t=PACK),
+            )
+            w_dealt.append(dealt)
+
+        sums = [psum.tile([P, J], F32, name="a%d" % t) for t in range(PACK)]
+        for a in range(PASSES):
+            for t in range(PACK):
+                cols = slice(t * P, (t + 1) * P)
+                nc.tensor.matmul_mx(
+                    out=sums[t][:],
+                    lhsT=w_dealt[a][:, cols].bitcast(E4M3),
+                    lhsT_scale=ws[:, a * R + t * P : a * R + (t + 1) * P],
+                    rhs=u_codes[a][:].bitcast(E4M3),
+                    rhs_scale=u_scales[a][:],
+                    start=(a == 0),
+                    stop=(a == PASSES - 1),
+                )
+
+        ha = [held([P, J], F32, "ha%d" % t) for t in range(PACK)]
+        nc.vector.tensor_scalar(ha[0][:], sums[0][:], 0.0, None, ALU.max)
+        nc.scalar.activation(ha[1][:], sums[1][:], ACT.Relu)
+        nc.vector.tensor_scalar(ha[3][:], sums[3][:], 0.0, None, ALU.max)
+        nc.vector.tensor_copy(placed[0][:].indirect(put[:]), ha[0][:])
+        nc.scalar.activation(placed[1][:].indirect(put[:]), ha[1][:], ACT.Copy)
+        nc.scalar.activation(ha[2][:], sums[2][:], ACT.Relu)
+        nc.scalar.activation(placed[2][:].indirect(put[:]), ha[2][:], ACT.Copy)
+        nc.scalar.activation(placed[3][:].indirect(put[:]), ha[3][:], ACT.Copy)
+
+        hid = held([P, PACK, O], F32, "hid")
+        pages = []
+        for t in range(PACK):
+            page = held([P, C], F32, "page%d" % t)
+            nc.vector.tensor_tensor(page[:], placed[t][:], old[t][:], ALU.add)
+            pages.append(page)
+        for t in range(PACK):
+            if t == PACK - 1:
+                nc.vector.tensor_copy(hid[:, t, :], pages[t][:].indirect(read[:]))
+            else:
+                nc.scalar.activation(hid[:, t, :], pages[t][:].indirect(read[:]), ACT.Copy)
+
+        hid_bf = held([P, O, PACK], BF16, "hid_bf")
+        interleave(nc, hid_bf, hid)
+        h_codes = held([P, O], U32, "h_codes")
+        h_scales = held([P, O], U8, "h_scales")
+        nc.vector.quantize_mx(
+            out=h_codes[:].bitcast(E5M2), scales=h_scales[:], in_=hid_bf[:].rearrange("p o t -> p (o t)")
+        )
+
+        y = held([P, PACK, O], F32, "y")
+        y_rows = out_0.rearrange("(p t) o -> p t o", t=PACK)
+        for t in range(PACK):
+            cols = slice(t * P, (t + 1) * P)
+            prod = psum.tile([P, O], F32, name="p%d" % t)
+            nc.tensor.matmul_mx(
+                out=prod[:],
+                lhsT=wb_dealt[:, cols].bitcast(E2M1),
+                lhsT_scale=wbs[:, cols],
+                rhs=h_codes[:].bitcast(E5M2),
+                rhs_scale=h_scales[:],
+                start=True,
+                stop=True,
+            )
+            nc.vector.scalar_tensor_tensor(
+                y[:, t, :], prod[:], gm_sb[:, t : t + 1], rs_sb[:, t, :], ALU.mult, ALU.add
+            )
+            if t % 2 == 1:
+                nc.sync.dma_start(y_rows[:, t - 1 : t + 1, :], y[:, t - 1 : t + 1, :])
+
+        y_bf = held([P, O, PACK], BF16, "y_bf")
+        interleave(nc, y_bf, y)
+        y_codes = held([P, O], U32, "y_codes")
+        y_scales = held([P, O], U8, "y_scales")
+        nc.vector.quantize_mx(
+            out=y_codes[:].bitcast(E4M3), scales=y_scales[:], in_=y_bf[:].rearrange("p o t -> p (o t)")
+        )
+        nc.sync.dma_start(out_1[0].rearrange("p c r -> p (c r)").bitcast(I32), y_codes[:].bitcast(I32))
+        for q in range(QUADS):
+            queue = nc.scalar if q % 2 == 0 else nc.sync
+            queue.dma_start(
+                out_2[0, 4 * q : 4 * q + 4, :].bitcast(I32), y_scales[32 * q : 32 * q + 4, :].bitcast(I32)
+            )

@@ -22,14 +22,17 @@ PACK = 4
 PASSES = K // (P * PACK)
 QUADS = 4
 WB_ROW, W_ROW = 96, 112
-VECTOR_PICKS = (0, 1, 2, 3, 5, 6)
+VECTOR_PICKS = (0, 1, 2, 3, 5)
+VECTOR_COLS = 160
 
 
 def interleave(nc, dst, src):
-    nc.vector.tensor_copy(
-        out=dst[:].rearrange("p (c i) t -> p c t i", i=4),
-        in_=src[:].rearrange("p t (c i) -> p c t i", i=4),
-    )
+    width = src.shape[2]
+    for copy, cols in ((nc.vector.tensor_copy, slice(0, VECTOR_COLS)), (nc.scalar.copy, slice(VECTOR_COLS, width))):
+        copy(
+            out=dst[:, cols, :].rearrange("p (c i) t -> p c t i", i=4),
+            in_=src[:, :, cols].rearrange("p t (c i) -> p c t i", i=4),
+        )
 
 
 def tile_list_page_largerpicks_residual_pl_kernel(
@@ -50,34 +53,33 @@ def tile_list_page_largerpicks_residual_pl_kernel(
         read = lists.tile([P, O // 16], U16, name="read")
 
         rows_raw = held([P, PASSES * R], U8, "rows_raw")
-        nc.vector.memset(rows_raw[0:WB_ROW, :].bitcast(U32), 0)
-        nc.vector.memset(rows_raw[WB_ROW:W_ROW, N:].bitcast(U32), 0)
+        nc.gpsimd.memset(rows_raw[0:WB_ROW, :].bitcast(U32), 0)
+        nc.gpsimd.memset(rows_raw[WB_ROW:W_ROW, N:].bitcast(U32), 0)
         nc.sync.dma_start(first[:], offs)
         nc.sync.dma_start(second[:], offs2)
-        wb_raw = held([P, N], U16, "wb_raw")
-        nc.scalar.dma_start(wb_raw[:].bitcast(I32), wb_words[0].bitcast(I32))
         nc.scalar.dma_start(
             rows_raw[W_ROW:P, :].bitcast(I32).rearrange("q (a c) -> q a c", a=PASSES),
             w_scales.bitcast(I32).rearrange("a q c -> q a c"),
         )
         nc.scalar.dma_start(rows_raw[WB_ROW:W_ROW, 0:N].bitcast(I32), wb_scales[0].bitcast(I32))
-        fk_sb = held([P, PASSES, PACK], F32, "fk_sb")
-        nc.scalar.dma_start(fk_sb[:], fk.rearrange("(a p t) o -> p a (t o)", p=P, t=PACK))
+        wb_raw = held([P, N], U16, "wb_raw")
+        nc.scalar.dma_start(wb_raw[:].bitcast(I32), wb_words[0].bitcast(I32))
         ws = held([P, PASSES * R], U8, "ws")
         wbs = held([P, N], U8, "wbs")
-        nc.gpsimd.memset(ws[:].bitcast(U32), 0)
-        nc.gpsimd.memset(wbs[:].bitcast(U32), 0)
         x_rows = xf.rearrange("(a p t) c -> a t p c", p=P, t=PACK)
+        fk_sb = held([P, PASSES, PACK], F32, "fk_sb")
         x_tiles = []
         for i in range(PASSES * PACK):
             x_tile = held([P, T], F32, "x%d" % i)
             nc.sync.dma_start(x_tile[:], x_rows[i // PACK, i % PACK])
             x_tiles.append(x_tile)
+            if i == 2:
+                nc.sync.dma_start(fk_sb[:], fk.rearrange("(a p t) o -> p a (t o)", p=P, t=PACK))
 
         placed = []
         for t in range(PACK):
             placed_tile = held([P, C], F32, "placed%d" % t)
-            (nc.vector if t < 2 else nc.gpsimd).memset(placed_tile[:], 0.0)
+            nc.gpsimd.memset(placed_tile[:], 0.0)
             placed.append(placed_tile)
 
         wb_dealt = held([P, N], U16, "wb_dealt")
@@ -87,18 +89,18 @@ def tile_list_page_largerpicks_residual_pl_kernel(
         )
         rows_dealt = held([P, PASSES * R], U8, "rows_dealt")
         nc.vector.tensor_copy(
-            out=rows_dealt[:].rearrange("p (a t m) -> p a m t", a=PASSES, t=PACK),
-            in_=rows_raw[:].rearrange("p (a m t) -> p a m t", a=PASSES, t=PACK),
+            out=rows_dealt[:].rearrange("p (a t m) -> p a t m", a=PASSES, t=PACK),
+            in_=rows_raw[:].rearrange("p (a m t) -> p a t m", a=PASSES, t=PACK),
         )
-        for q in range(QUADS):
-            nc.sync.dma_start(
-                ws[32 * q : 32 * q + 4, :].bitcast(I32), rows_dealt[W_ROW + 4 * q : W_ROW + 4 * q + 4, :].bitcast(I32)
-            )
         w_raw = []
         for a in range(PASSES):
             w_tile = held([P, R], U32, "w_raw%d" % a)
             nc.sync.dma_start(w_tile[:].bitcast(I32), w_words[a].rearrange("p c r -> p (c r)").bitcast(I32))
             w_raw.append(w_tile)
+        for q in range(QUADS):
+            nc.sync.dma_start(
+                ws[32 * q : 32 * q + 4, :].bitcast(I32), rows_dealt[W_ROW + 4 * q : W_ROW + 4 * q + 4, :].bitcast(I32)
+            )
         nc.sync.dma_start(put[:], offs3)
         old_rows = oldh.rearrange("(p t) c -> t p c", t=PACK)
         old = []
@@ -193,7 +195,8 @@ def tile_list_page_largerpicks_residual_pl_kernel(
             pages.append(page)
         for t in range(PACK):
             if t == PACK - 1:
-                nc.vector.tensor_copy(hid[:, t, :], pages[t][:].indirect(read[:]))
+                nc.vector.tensor_copy(hid[:, t, 0 : O // 2], pages[t][:].indirect(read[:, 0 : O // 32]))
+                nc.scalar.activation(hid[:, t, O // 2 : O], pages[t][:].indirect(read[:, O // 32 : O // 16]), ACT.Copy)
             else:
                 nc.scalar.activation(hid[:, t, :], pages[t][:].indirect(read[:]), ACT.Copy)
 

from contextlib import ExitStack

import concourse.mybir as mybir

K, T, J, R, C, O, N = 1024, 1024, 256, 512, 1024, 256, 512
FLOPS = 2 * K * R * J + 2 * R * N * O

F32 = mybir.dt.float32
BF16 = mybir.dt.bfloat16
I32 = mybir.dt.int32
U32 = mybir.dt.uint32
U16 = mybir.dt.uint16
U8 = mybir.dt.uint8
E4M3 = mybir.dt.float8_e4m3fn_x4
E5M2 = mybir.dt.float8_e5m2_x4
E2M1 = mybir.dt.float4_e2m1fn_x4
ALU = mybir.AluOpType
ACT = mybir.ActivationFunctionType

P = 128
PACK = 4
PASSES = K // (P * PACK)
QUADS = 4
WB_ROW, W_ROW = 96, 112
VECTOR_PICKS = (0, 1, 2, 3, 5)
VECTOR_COLS = 160


def interleave(nc, dst, src):
    width = src.shape[2]
    for copy, cols in ((nc.vector.tensor_copy, slice(0, VECTOR_COLS)), (nc.scalar.copy, slice(VECTOR_COLS, width))):
        copy(
            out=dst[:, cols, :].rearrange("p (c i) t -> p c t i", i=4),
            in_=src[:, :, cols].rearrange("p t (c i) -> p c t i", i=4),
        )


def tile_list_page_largerpicks_residual_pl_kernel(
    tc, xf, fk, w_words, w_scales, oldh, wb_words, wb_scales, rs, gm, offs, offs2, offs3, offs4, out_0, out_1, out_2
):
    nc = tc.nc
    with ExitStack() as ctx:
        lists = ctx.enter_context(tc.tile_pool(name="lists", bufs=1))
        keep = ctx.enter_context(tc.tile_pool(name="keep", bufs=1))
        psum = ctx.enter_context(tc.psum_pool(name="psum", bufs=1))

        def held(shape, dtype, name):
            return keep.tile(shape, dtype, name=name, align_bytes=64)

        first = lists.tile([P, J // 16], U16, name="first")
        second = lists.tile([P, J // 16], U16, name="second")
        put = lists.tile([P, J // 16], U16, name="put")
        read = lists.tile([P, O // 16], U16, name="read")

        rows_raw = held([P, PASSES * R], U8, "rows_raw")
        nc.gpsimd.memset(rows_raw[0:WB_ROW, :].bitcast(U32), 0)
        nc.gpsimd.memset(rows_raw[WB_ROW:W_ROW, N:].bitcast(U32), 0)
        nc.sync.dma_start(first[:], offs)
        nc.sync.dma_start(second[:], offs2)
        nc.scalar.dma_start(
            rows_raw[W_ROW:P, :].bitcast(I32).rearrange("q (a c) -> q a c", a=PASSES),
            w_scales.bitcast(I32).rearrange("a q c -> q a c"),
        )
        nc.scalar.dma_start(rows_raw[WB_ROW:W_ROW, 0:N].bitcast(I32), wb_scales[0].bitcast(I32))
        wb_raw = held([P, N], U16, "wb_raw")
        nc.scalar.dma_start(wb_raw[:].bitcast(I32), wb_words[0].bitcast(I32))
        ws = held([P, PASSES * R], U8, "ws")
        wbs = held([P, N], U8, "wbs")
        x_rows = xf.rearrange("(a p t) c -> a t p c", p=P, t=PACK)
        fk_sb = held([P, PASSES, PACK], F32, "fk_sb")
        x_tiles = []
        for i in range(PASSES * PACK):
            x_tile = held([P, T], F32, "x%d" % i)
            nc.sync.dma_start(x_tile[:], x_rows[i // PACK, i % PACK])
            x_tiles.append(x_tile)
            if i == 2:
                nc.sync.dma_start(fk_sb[:], fk.rearrange("(a p t) o -> p a (t o)", p=P, t=PACK))

        placed = []
        for t in range(PACK):
            placed_tile = held([P, C], F32, "placed%d" % t)
            nc.gpsimd.memset(placed_tile[:], 0.0)
            placed.append(placed_tile)

        wb_dealt = held([P, N], U16, "wb_dealt")
        nc.scalar.copy(
            out=wb_dealt[:].rearrange("p (t m) -> p m t", t=PACK),
            in_=wb_raw[:].rearrange("p (m t) -> p m t", t=PACK),
        )
        rows_dealt = held([P, PASSES * R], U8, "rows_dealt")
        nc.vector.tensor_copy(
            out=rows_dealt[:].rearrange("p (a t m) -> p a t m", a=PASSES, t=PACK),
            in_=rows_raw[:].rearrange("p (a m t) -> p a t m", a=PASSES, t=PACK),
        )
        w_raw = []
        for a in range(PASSES):
            w_tile = held([P, R], U32, "w_raw%d" % a)
            nc.sync.dma_start(w_tile[:].bitcast(I32), w_words[a].rearrange("p c r -> p (c r)").bitcast(I32))
            w_raw.append(w_tile)
        for q in range(QUADS):
            nc.sync.dma_start(
                ws[32 * q : 32 * q + 4, :].bitcast(I32), rows_dealt[W_ROW + 4 * q : W_ROW + 4 * q + 4, :].bitcast(I32)
            )
        nc.sync.dma_start(put[:], offs3)
        old_rows = oldh.rearrange("(p t) c -> t p c", t=PACK)
        old = []
        for t in range(PACK):
            old_tile = held([P, C], F32, "old%d" % t)
            nc.sync.dma_start(old_tile[:], old_rows[t])
            old.append(old_tile)
        nc.sync.dma_start(read[:], offs4)
        for q in range(QUADS):
            nc.sync.dma_start(
                wbs[32 * q : 32 * q + 4, :].bitcast(I32), rows_dealt[WB_ROW + 4 * q : WB_ROW + 4 * q + 4, 0:N].bitcast(I32)
            )

        gm_sb = held([P, PACK], F32, "gm_sb")
        nc.sync.dma_start(gm_sb[:], gm.rearrange("(p t) o -> p (t o)", t=PACK))
        rs_sb = held([P, PACK, O], F32, "rs_sb")
        nc.sync.dma_start(rs_sb[:], rs.rearrange("(p t) o -> p t o", t=PACK))

        u_codes, u_scales = [], []
        for a in range(PASSES):
            u_bf = held([P, J, PACK], BF16, "u_bf%d" % a)
            pick1 = held([P, PACK, J], F32, "pick1_%d" % a)
            pick2 = held([P, PACK, J], F32, "pick2_%d" % a)
            larger = held([P, PACK, J], F32, "larger%d" % a)
            last = a == PASSES - 1
            max_groups = ((0, 2), (2, 3), (3, 4)) if last else ((0, 2), (2, 4))
            joint = PACK - 1 if last else PACK
            for lo, hi in max_groups:
                for t in range(lo, hi):
                    i = a * PACK + t
                    nc.scalar.activation(pick1[:, t, :], x_tiles[i][:].indirect(first[:]), ACT.Copy)
                    if i in VECTOR_PICKS:
                        nc.vector.tensor_copy(pick2[:, t, :], x_tiles[i][:].indirect(second[:]))
                    else:
                        nc.scalar.activation(pick2[:, t, :], x_tiles[i][:].indirect(second[:]), ACT.Copy)
                nc.vector.tensor_tensor(larger[:, lo:hi, :], pick1[:, lo:hi, :], pick2[:, lo:hi, :], ALU.max)
                if hi == joint:
                    nc.vector.tensor_tensor(
                        u_bf[:, :, 0:joint].rearrange("p (c i) t -> p c t i", i=4),
                        larger[:, 0:joint, :].rearrange("p t (c i) -> p c t i", i=4),
                        fk_sb[:, a, 0:joint].unsqueeze(1).unsqueeze(3).to_broadcast([P, J // 4, joint, 4]),
                        ALU.mult,
                    )
                elif hi > joint:
                    nc.vector.tensor_scalar(u_bf[:, :, lo], larger[:, lo, :], fk_sb[:, a, lo:hi], None, ALU.mult)
            codes = held([P, J], U32, "u_codes%d" % a)
            scales = held([P, J], U8, "u_scales%d" % a)
            nc.vector.quantize_mx(
                out=codes[:].bitcast(E4M3), scales=scales[:], in_=u_bf[:].rearrange("p j t -> p (j t)")
            )
            u_codes.append(codes)
            u_scales.append(scales)

        w_dealt = []
        for a in range(PASSES):
            dealt = held([P, R], U32, "w_dealt%d" % a)
            nc.scalar.copy(
                out=dealt[:].rearrange("p (t m) -> p m t", t=PACK),
                in_=w_raw[a][:].rearrange("p (m t) -> p m t", t=PACK),
            )
            w_dealt.append(dealt)

        sums = [psum.tile([P, J], F32, name="a%d" % t) for t in range(PACK)]
        for a in range(PASSES):
            for t in range(PACK):
                cols = slice(t * P, (t + 1) * P)
                nc.tensor.matmul_mx(
                    out=sums[t][:],
                    lhsT=w_dealt[a][:, cols].bitcast(E4M3),
                    lhsT_scale=ws[:, a * R + t * P : a * R + (t + 1) * P],
                    rhs=u_codes[a][:].bitcast(E4M3),
                    rhs_scale=u_scales[a][:],
                    start=(a == 0),
                    stop=(a == PASSES - 1),
                )

        ha = [held([P, J], F32, "ha%d" % t) for t in range(PACK)]
        nc.vector.tensor_scalar(ha[0][:], sums[0][:], 0.0, None, ALU.max)
        nc.scalar.activation(ha[1][:], sums[1][:], ACT.Relu)
        nc.vector.tensor_scalar(ha[3][:], sums[3][:], 0.0, None, ALU.max)
        nc.vector.tensor_copy(placed[0][:].indirect(put[:]), ha[0][:])
        nc.scalar.activation(placed[1][:].indirect(put[:]), ha[1][:], ACT.Copy)
        nc.scalar.activation(ha[2][:], sums[2][:], ACT.Relu)
        nc.scalar.activation(placed[2][:].indirect(put[:]), ha[2][:], ACT.Copy)
        nc.scalar.activation(placed[3][:].indirect(put[:]), ha[3][:], ACT.Copy)

        hid = held([P, PACK, O], F32, "hid")
        pages = []
        for t in range(PACK):
            page = held([P, C], F32, "page%d" % t)
            nc.vector.tensor_tensor(page[:], placed[t][:], old[t][:], ALU.add)
            pages.append(page)
        for t in range(PACK):
            if t == PACK - 1:
                nc.vector.tensor_copy(hid[:, t, 0 : O // 2], pages[t][:].indirect(read[:, 0 : O // 32]))
                nc.scalar.activation(hid[:, t, O // 2 : O], pages[t][:].indirect(read[:, O // 32 : O // 16]), ACT.Copy)
            else:
                nc.scalar.activation(hid[:, t, :], pages[t][:].indirect(read[:]), ACT.Copy)

        hid_bf = held([P, O, PACK], BF16, "hid_bf")
        interleave(nc, hid_bf, hid)
        h_codes = held([P, O], U32, "h_codes")
        h_scales = held([P, O], U8, "h_scales")
        nc.vector.quantize_mx(
            out=h_codes[:].bitcast(E5M2), scales=h_scales[:], in_=hid_bf[:].rearrange("p o t -> p (o t)")
        )

        y = held([P, PACK, O], F32, "y")
        y_rows = out_0.rearrange("(p t) o -> p t o", t=PACK)
        for t in range(PACK):
            cols = slice(t * P, (t + 1) * P)
            prod = psum.tile([P, O], F32, name="p%d" % t)
            nc.tensor.matmul_mx(
                out=prod[:],
                lhsT=wb_dealt[:, cols].bitcast(E2M1),
                lhsT_scale=wbs[:, cols],
                rhs=h_codes[:].bitcast(E5M2),
                rhs_scale=h_scales[:],
                start=True,
                stop=True,
            )
            nc.vector.scalar_tensor_tensor(
                y[:, t, :], prod[:], gm_sb[:, t : t + 1], rs_sb[:, t, :], ALU.mult, ALU.add
            )
            if t % 2 == 1:
                nc.sync.dma_start(y_rows[:, t - 1 : t + 1, :], y[:, t - 1 : t + 1, :])

        y_bf = held([P, O, PACK], BF16, "y_bf")
        interleave(nc, y_bf, y)
        y_codes = held([P, O], U32, "y_codes")
        y_scales = held([P, O], U8, "y_scales")
        nc.vector.quantize_mx(
            out=y_codes[:].bitcast(E4M3), scales=y_scales[:], in_=y_bf[:].rearrange("p o t -> p (o t)")
        )
        nc.sync.dma_start(out_1[0].rearrange("p c r -> p (c r)").bitcast(I32), y_codes[:].bitcast(I32))
        for q in range(QUADS):
            queue = nc.scalar if q % 2 == 0 else nc.sync
            queue.dma_start(
                out_2[0, 4 * q : 4 * q + 4, :].bitcast(I32), y_scales[32 * q : 32 * q + 4, :].bitcast(I32)
            )
